import numpy as np
import ml_dtypes


def mxq(x, axis, fmt="e4m3"):
    dtype, down = {"e4m3": (ml_dtypes.float8_e4m3fn, 7), "e5m2": (ml_dtypes.float8_e5m2, 14)}[fmt]
    v = np.moveaxis(np.asarray(x, np.float32).astype(ml_dtypes.bfloat16).astype(np.float64), axis, -1)
    blocks = v.reshape(v.shape[:-1] + (-1, 32))
    amax = np.abs(blocks).max(-1, keepdims=True)
    byte = np.maximum(np.where(amax > 0, np.frexp(amax)[1] - 1 + 127, 0) - down, 1)
    scale = np.exp2(byte - 127.0)
    codes = (blocks / scale).astype(np.float32).astype(dtype).astype(np.float64)
    return np.moveaxis((codes * scale).reshape(v.shape), -1, axis)


WIDE = False


def mx_kscale(k):
    if not WIDE:
        return np.ones(k)
    levels = np.array([10, -10, 5, -5, 0])
    if k % 512:
        return np.exp2(np.random.permutation(np.resize(levels, k // 32))).repeat(32)
    a = np.empty((k // 512, 16))
    for p in range(k // 512):
        a[p, :8] = np.random.permutation(np.resize(levels, 8))
        for g in range(8):
            far = levels[np.abs(levels - a[p, g]) >= 10]
            a[p, g + 8] = far[np.random.randint(len(far))]
    return np.exp2(a.ravel()).repeat(32)


def f64(x):
    return np.asarray(x).astype(np.float64)


def striped(idx):
    return np.tile(np.asarray(idx).reshape(-1, 16).T, (8, 1)).astype(np.uint16)


def unstriped(offs):
    return offs[:16].T.reshape(-1).astype(np.int64)

def silu(v):
    return v / (1.0 + np.exp(-v))


B, N, T, D, NQ = 1, 512, 2048, 512, 256
DV = 512


def setup_inputs():
    n = np.random.standard_normal
    idx = np.random.permutation(T)[:B * N]
    u = mx_kscale(N)
    ut = np.ones(T)
    ut[idx] = u
    return {
        "vT": (n((DV, T)) / ut).astype(np.float32),
        "wT": (np.random.dirichlet(np.ones(N), NQ).T[None] * u[:, None] * 16).astype(np.float32),
        "ob": (0.5 * n((B, 1, DV))).astype(np.float32),
        "offs": striped(idx),
    }


def reference(vT, wT, ob, offs):
    idx = unstriped(offs)
    pick = lambda x, which: x[:, which].reshape(x.shape[0], B, -1).transpose(1, 0, 2)
    wq = mxq(f64(wT), 1, "e4m3")
    o = wq.transpose(0, 2, 1) @ mxq(pick(f64(vT), idx).transpose(0, 2, 1), 1, "e4m3")
    r_ = silu(o + f64(ob))
    return r_

@@ -1,0 +1,137 @@
+from contextlib import ExitStack
+
+import concourse.mybir as mybir
+from concourse.masks import make_identity
+
+F32 = mybir.dt.float32
+BF16 = mybir.dt.bfloat16
+U32 = mybir.dt.uint32
+U16 = mybir.dt.uint16
+U8 = mybir.dt.uint8
+FP8X4 = mybir.dt.float8_e4m3fn_x4
+SILU = mybir.ActivationFunctionType.Silu
+ADD = mybir.AluOpType.add
+
+P = 128
+PACK = 4
+SLOTS, TOKENS, QUERIES, FEATURES = 512, 2048, 256, 512
+BLOCKS = FEATURES // P
+HALVES = QUERIES // P
+WINDOW_BYTES = TOKENS * 4
+LAST = BLOCKS - 1
+
+FLOPS = 2 * SLOTS * QUERIES * FEATURES
+
+
+def tile_attend_wsum_silu_f_topk_kernel(tc, vT, wT, ob, offs, out):
+    nc = tc.nc
+    with ExitStack() as ctx:
+        keep = ctx.enter_context(tc.tile_pool(name="keep", bufs=1))
+        placed = ctx.enter_context(tc.tile_pool(name="placed", bufs=1))
+        psum = ctx.enter_context(tc.psum_pool(name="psum", bufs=1))
+
+        offsets = keep.tile([P, SLOTS // 16], U16, name="offsets")
+        windows = [
+            placed.tile([P, TOKENS], F32, name=f"window{b}", offset=b * WINDOW_BYTES, align_bytes=64)
+            for b in range(BLOCKS)
+        ]
+        w_raw = keep.tile([P, PACK, QUERIES], F32, name="w_raw")
+        bias_col = keep.tile([P, PACK], F32, name="bias_col")
+
+        nc.sync.dma_start(windows[0][:], vT[0:P, :])
+        nc.sync.dma_start(offsets[:], offs)
+        nc.sync.dma_start(bias_col[:], ob[0, 0].rearrange("(p c) -> p c", c=PACK))
+        nc.sync.dma_start(w_raw[:], wT[0].rearrange("(p j) q -> p j q", j=PACK))
+        for b in range(1, BLOCKS):
+            nc.sync.dma_start(windows[b][:], vT[b * P : (b + 1) * P, :])
+
+        ident = keep.tile([P, P], F32, name="ident")
+        make_identity(nc, ident[:])
+
+        out_rows = out[0].rearrange("(h p) e -> p h e", p=P)
+
+        w_codes = keep.tile([P, QUERIES], U32, name="w_codes", align_bytes=64)
+        w_scales = keep.tile([P, QUERIES], U8, name="w_scales", align_bytes=64)
+        bias_rows = keep.tile([P, P, PACK], F32, name="bias_rows")
+
+        def prepare_bias():
+            bias_ps = psum.tile([P, PACK, P], F32, name="bias_ps")
+            for c in range(PACK):
+                nc.tensor.transpose(bias_ps[:, c, :], bias_col[:, c : c + 1].to_broadcast([P, P]), ident[:])
+            nc.scalar.copy(bias_rows[:], bias_ps[:].rearrange("q c n -> q n c"))
+
+        def prepare_weights():
+            w_grouped = keep.tile([P, QUERIES, PACK], BF16, name="w_grouped", align_bytes=64)
+            nc.scalar.copy(w_grouped[:], w_raw[:].rearrange("p j q -> p q j"))
+            nc.vector.quantize_mx(
+                out=w_codes[:].bitcast(FP8X4),
+                scales=w_scales[:],
+                in_=w_grouped[:].rearrange("p q j -> p (q j)"),
+            )
+
+        def gather_and_turn(b):
+            picked = keep.tile([P, 2, P, 2], BF16, name=f"picked{b}", tag=f"picked{b}", align_bytes=64)
+            nc.vector.tensor_copy(
+                picked[:].rearrange("e u p v -> e p u v"), windows[b][:].indirect(offsets[:])
+            )
+            words = picked[:].rearrange("e u p v -> e (u p v)").bitcast(F32)
+            turned = psum.tile([P, 2, P], F32, name=f"turned{b % 2}")
+            for u in range(2):
+                nc.tensor.transpose(turned[:, u, :], words[:, u * P : (u + 1) * P], ident[:])
+            v_grouped = keep.tile([P, P * PACK], BF16, name=f"v_grouped{b}", tag=f"v_grouped{b}", align_bytes=64)
+            nc.scalar.copy(
+                v_grouped[:].bitcast(F32).rearrange("p (e u) -> p e u", u=2),
+                turned[:].rearrange("p u e -> p e u"),
+            )
+            return v_grouped
+
+        def multiply(b, v_grouped):
+            if b < LAST:
+                v_codes = placed.tile([P, P], U32, name=f"v_codes{b}", offset=(b + 1) * WINDOW_BYTES, align_bytes=64)
+            else:
+                v_codes = keep.tile([P, P], U32, name=f"v_codes{b}", align_bytes=64)
+            v_scales = keep.tile([P, P], U8, name=f"v_scales{b}", align_bytes=64)
+            nc.vector.quantize_mx(out=v_codes[:].bitcast(FP8X4), scales=v_scales[:], in_=v_grouped[:])
+            acc = psum.tile([P, HALVES, P], F32, name=f"acc{b}")
+            for h in range(HALVES):
+                cols = slice(h * P, (h + 1) * P)
+                nc.tensor.matmul_mx(
+                    out=acc[:, h, :],
+                    lhsT=w_codes[:, cols].bitcast(FP8X4),
+                    lhsT_scale=w_scales[:, cols],
+                    rhs=v_codes[:].bitcast(FP8X4),
+                    rhs_scale=v_scales[:],
+                    start=True,
+                    stop=True,
+                )
+            return acc
+
+        def finish(b, acc):
+            bias = bias_rows[:].rearrange("q n c -> q (n c)")[:, b * P : (b + 1) * P]
+            if b + 2 <= LAST:
+                summed = placed.tile(
+                    [P, HALVES, P], F32, name=f"summed{b}", offset=(b + 2) * WINDOW_BYTES + 1024, align_bytes=64
+                )
+            elif b + 1 == LAST:
+                summed = keep.tile([P, HALVES, P], F32, name=f"summed{b}", tag=f"v_grouped{LAST}", align_bytes=64)
+            else:
+                summed = keep.tile([P, HALVES, P], F32, name=f"summed{b}")
+            nc.vector.tensor_tensor(summed[:], acc[:], bias.unsqueeze(1).to_broadcast([P, HALVES, P]), ADD)
+            if b + 2 == LAST:
+                result = keep.tile([P, HALVES, P], F32, name=f"result{b}", tag=f"picked{LAST}", align_bytes=64)
+            else:
+                result = keep.tile([P, HALVES, P], F32, name=f"result{b}")
+            nc.scalar.activation(result[:], summed[:], SILU)
+            nc.sync.dma_start(out_rows[:, :, b * P : (b + 1) * P], result[:])
+
+        grouped = {0: gather_and_turn(0)}
+        prepare_bias()
+        prepare_weights()
+        sums = {}
+        for step in range(1, BLOCKS + 2):
+            if step < BLOCKS:
+                grouped[step] = gather_and_turn(step)
+            if step - 1 < BLOCKS:
+                sums[step - 1] = multiply(step - 1, grouped[step - 1])
+            if step >= 2:
+                finish(step - 2, sums[step - 2])

@@ -18,7 +18,7 @@ SLOTS, TOKENS, QUERIES, FEATURES = 512, 2048, 256, 512
 BLOCKS = FEATURES // P
 HALVES = QUERIES // P
 WINDOW_BYTES = TOKENS * 4
-LAST = BLOCKS - 1
+W_OFFSET = BLOCKS * WINDOW_BYTES
 
 FLOPS = 2 * SLOTS * QUERIES * FEATURES
 
@@ -35,42 +35,29 @@ def tile_attend_wsum_silu_f_topk_kernel(tc, vT, wT, ob, offs, out):
             placed.tile([P, TOKENS], F32, name=f"window{b}", offset=b * WINDOW_BYTES, align_bytes=64)
             for b in range(BLOCKS)
         ]
-        w_raw = keep.tile([P, PACK, QUERIES], F32, name="w_raw")
+        w_raw = placed.tile([P, PACK, QUERIES], F32, name="w_raw", offset=W_OFFSET, align_bytes=64)
         bias_col = keep.tile([P, PACK], F32, name="bias_col")
 
+        nc.scalar.dma_start(bias_col[:], ob[0, 0].rearrange("(p c) -> p c", c=PACK))
         nc.sync.dma_start(windows[0][:], vT[0:P, :])
         nc.sync.dma_start(offsets[:], offs)
-        nc.sync.dma_start(bias_col[:], ob[0, 0].rearrange("(p c) -> p c", c=PACK))
-        nc.sync.dma_start(w_raw[:], wT[0].rearrange("(p j) q -> p j q", j=PACK))
         for b in range(1, BLOCKS):
             nc.sync.dma_start(windows[b][:], vT[b * P : (b + 1) * P, :])
+        nc.sync.dma_start(w_raw[:], wT[0].rearrange("(p j) q -> p j q", j=PACK))
 
         ident = keep.tile([P, P], F32, name="ident")
         make_identity(nc, ident[:])
+        warm = keep.tile([P, 1], F32, name="warm")
+        nc.scalar.activation(warm[:], ident[:, 0:1], SILU)
 
-        out_rows = out[0].rearrange("(h p) e -> p h e", p=P)
+        bias_ps = psum.tile([P, PACK, P], F32, name="bias_ps")
+        for c in range(PACK):
+            nc.tensor.transpose(bias_ps[:, c, :], bias_col[:, c : c + 1].to_broadcast([P, P]), ident[:])
+        bias_rows = keep.tile([P, FEATURES], F32, name="bias_rows")
+        nc.scalar.copy(bias_rows[:].rearrange("q (n c) -> q n c", c=PACK), bias_ps[:].rearrange("q c n -> q n c"))
 
-        w_codes = keep.tile([P, QUERIES], U32, name="w_codes", align_bytes=64)
-        w_scales = keep.tile([P, QUERIES], U8, name="w_scales", align_bytes=64)
-        bias_rows = keep.tile([P, P, PACK], F32, name="bias_rows")
-
-        def prepare_bias():
-            bias_ps = psum.tile([P, PACK, P], F32, name="bias_ps")
-            for c in range(PACK):
-                nc.tensor.transpose(bias_ps[:, c, :], bias_col[:, c : c + 1].to_broadcast([P, P]), ident[:])
-            nc.scalar.copy(bias_rows[:], bias_ps[:].rearrange("q c n -> q n c"))
-
-        def prepare_weights():
-            w_grouped = keep.tile([P, QUERIES, PACK], BF16, name="w_grouped", align_bytes=64)
-            nc.scalar.copy(w_grouped[:], w_raw[:].rearrange("p j q -> p q j"))
-            nc.vector.quantize_mx(
-                out=w_codes[:].bitcast(FP8X4),
-                scales=w_scales[:],
-                in_=w_grouped[:].rearrange("p q j -> p (q j)"),
-            )
-
-        def gather_and_turn(b):
-            picked = keep.tile([P, 2, P, 2], BF16, name=f"picked{b}", tag=f"picked{b}", align_bytes=64)
+        def gather_and_turn(b, grouped):
+            picked = keep.tile([P, 2, P, 2], BF16, name=f"picked{b}", align_bytes=64)
             nc.vector.tensor_copy(
                 picked[:].rearrange("e u p v -> e p u v"), windows[b][:].indirect(offsets[:])
             )
@@ -78,60 +65,68 @@ def tile_attend_wsum_silu_f_topk_kernel(tc, vT, wT, ob, offs, out):
             turned = psum.tile([P, 2, P], F32, name=f"turned{b % 2}")
             for u in range(2):
                 nc.tensor.transpose(turned[:, u, :], words[:, u * P : (u + 1) * P], ident[:])
-            v_grouped = keep.tile([P, P * PACK], BF16, name=f"v_grouped{b}", tag=f"v_grouped{b}", align_bytes=64)
             nc.scalar.copy(
-                v_grouped[:].bitcast(F32).rearrange("p (e u) -> p e u", u=2),
+                grouped.bitcast(F32).rearrange("p (e u) -> p e u", u=2),
                 turned[:].rearrange("p u e -> p e u"),
             )
-            return v_grouped
 
-        def multiply(b, v_grouped):
-            if b < LAST:
-                v_codes = placed.tile([P, P], U32, name=f"v_codes{b}", offset=(b + 1) * WINDOW_BYTES, align_bytes=64)
+        def quantize(name, grouped, width, offset):
+            if offset is None:
+                codes = keep.tile([P, width], U32, name=f"{name}_codes", align_bytes=64)
             else:
-                v_codes = keep.tile([P, P], U32, name=f"v_codes{b}", align_bytes=64)
-            v_scales = keep.tile([P, P], U8, name=f"v_scales{b}", align_bytes=64)
-            nc.vector.quantize_mx(out=v_codes[:].bitcast(FP8X4), scales=v_scales[:], in_=v_grouped[:])
+                codes = placed.tile([P, width], U32, name=f"{name}_codes", offset=offset, align_bytes=64)
+            scales = keep.tile([P, width], U8, name=f"{name}_scales", align_bytes=64)
+            nc.vector.quantize_mx(out=codes[:].bitcast(FP8X4), scales=scales[:], in_=grouped)
+            return codes, scales
+
+        def multiply(acc, w, v):
+            nc.tensor.matmul_mx(
+                out=acc,
+                lhsT=w[0][:].bitcast(FP8X4),
+                lhsT_scale=w[1][:],
+                rhs=v[0][:].bitcast(FP8X4),
+                rhs_scale=v[1][:],
+                start=True,
+                stop=True,
+            )
+
+        grouped01 = keep.tile([P, 2 * P * PACK], BF16, name="grouped01", align_bytes=64)
+        grouped2 = keep.tile([P, P * PACK], BF16, name="grouped2", align_bytes=64)
+        gather_and_turn(0, grouped01[:, : P * PACK])
+        gather_and_turn(1, grouped01[:, P * PACK :])
+        gather_and_turn(2, grouped2[:])
+        v01 = quantize("v01", grouped01[:], 2 * P, 2 * WINDOW_BYTES)
+
+        w_grouped = [keep.tile([P, P, PACK], BF16, name=f"w_grouped{h}", align_bytes=64) for h in range(HALVES)]
+        w_read = w_raw[:].rearrange("p j q -> p q j")
+        nc.scalar.copy(w_grouped[1][:], w_read[:, P:, :])
+        nc.vector.tensor_copy(w_grouped[0][:], w_read[:, :P, :])
+
+        grouped3 = placed.tile([P, P * PACK], BF16, name="grouped3", offset=W_OFFSET, align_bytes=64)
+        gather_and_turn(3, grouped3[:])
+        w = [quantize(f"w{h}", w_grouped[h][:].rearrange("p q j -> p (q j)"), P, None) for h in range(HALVES)]
+        v2 = quantize("v2", grouped2[:], P, W_OFFSET + 2048)
+        v3 = quantize("v3", grouped3[:], P, None)
+
+        out_rows = out[0].rearrange("(h p) e -> p h e", p=P)
+        units = []
+        for h in range(HALVES):
+            acc = psum.tile([P, 2 * P], F32, name=f"acc{h}")
+            multiply(acc[:], w[h], v01)
+            units.append((acc[:], bias_rows[:, : 2 * P], out_rows[:, h, : 2 * P]))
+        for b, v in ((2, v2), (3, v3)):
             acc = psum.tile([P, HALVES, P], F32, name=f"acc{b}")
             for h in range(HALVES):
-                cols = slice(h * P, (h + 1) * P)
-                nc.tensor.matmul_mx(
-                    out=acc[:, h, :],
-                    lhsT=w_codes[:, cols].bitcast(FP8X4),
-                    lhsT_scale=w_scales[:, cols],
-                    rhs=v_codes[:].bitcast(FP8X4),
-                    rhs_scale=v_scales[:],
-                    start=True,
-                    stop=True,
-                )
-            return acc
+                multiply(acc[:, h, :], w[h], v)
+            cols = slice(b * P, (b + 1) * P)
+            units.append((acc[:], bias_rows[:, cols].unsqueeze(1).to_broadcast([P, HALVES, P]), out_rows[:, :, cols]))
 
-        def finish(b, acc):
-            bias = bias_rows[:].rearrange("q n c -> q (n c)")[:, b * P : (b + 1) * P]
-            if b + 2 <= LAST:
-                summed = placed.tile(
-                    [P, HALVES, P], F32, name=f"summed{b}", offset=(b + 2) * WINDOW_BYTES + 1024, align_bytes=64
-                )
-            elif b + 1 == LAST:
-                summed = keep.tile([P, HALVES, P], F32, name=f"summed{b}", tag=f"v_grouped{LAST}", align_bytes=64)
+        for n, (acc, bias, dest) in enumerate(units):
+            if n == 0:
+                summed = placed.tile(list(acc.shape), F32, name="summed0", offset=W_OFFSET, align_bytes=64)
             else:
-                summed = keep.tile([P, HALVES, P], F32, name=f"summed{b}")
-            nc.vector.tensor_tensor(summed[:], acc[:], bias.unsqueeze(1).to_broadcast([P, HALVES, P]), ADD)
-            if b + 2 == LAST:
-                result = keep.tile([P, HALVES, P], F32, name=f"result{b}", tag=f"picked{LAST}", align_bytes=64)
-            else:
-                result = keep.tile([P, HALVES, P], F32, name=f"result{b}")
+                summed = keep.tile(list(acc.shape), F32, name=f"summed{n}")
+            nc.vector.tensor_tensor(summed[:], acc, bias, ADD)
+            result = keep.tile(list(acc.shape), F32, name=f"result{n}")
             nc.scalar.activation(result[:], summed[:], SILU)
-            nc.sync.dma_start(out_rows[:, :, b * P : (b + 1) * P], result[:])
-
-        grouped = {0: gather_and_turn(0)}
-        prepare_bias()
-        prepare_weights()
-        sums = {}
-        for step in range(1, BLOCKS + 2):
-            if step < BLOCKS:
-                grouped[step] = gather_and_turn(step)
-            if step - 1 < BLOCKS:
-                sums[step - 1] = multiply(step - 1, grouped[step - 1])
-            if step >= 2:
-                finish(step - 2, sums[step - 2])
+            nc.sync.dma_start(dest, result[:])

@@ -99,8 +99,9 @@ def tile_attend_wsum_silu_f_topk_kernel(tc, vT, wT, ob, offs, out):
 
         w_grouped = [keep.tile([P, P, PACK], BF16, name=f"w_grouped{h}", align_bytes=64) for h in range(HALVES)]
         w_read = w_raw[:].rearrange("p j q -> p q j")
-        nc.scalar.copy(w_grouped[1][:], w_read[:, P:, :])
-        nc.vector.tensor_copy(w_grouped[0][:], w_read[:, :P, :])
+        for h, split in enumerate((80, 64)):
+            nc.vector.tensor_copy(w_grouped[h][:, :split, :], w_read[:, h * P : h * P + split, :])
+            nc.scalar.copy(w_grouped[h][:, split:, :], w_read[:, h * P + split : (h + 1) * P, :])
 
         grouped3 = placed.tile([P, P * PACK], BF16, name="grouped3", offset=W_OFFSET, align_bytes=64)
         gather_and_turn(3, grouped3[:])
@@ -114,12 +115,12 @@ def tile_attend_wsum_silu_f_topk_kernel(tc, vT, wT, ob, offs, out):
             acc = psum.tile([P, 2 * P], F32, name=f"acc{h}")
             multiply(acc[:], w[h], v01)
             units.append((acc[:], bias_rows[:, : 2 * P], out_rows[:, h, : 2 * P]))
-        for b, v in ((2, v2), (3, v3)):
-            acc = psum.tile([P, HALVES, P], F32, name=f"acc{b}")
+        late = [psum.tile([P, 2 * P], F32, name=f"late{h}") for h in range(HALVES)]
+        for cols, v in ((slice(0, P), v2), (slice(P, 2 * P), v3)):
             for h in range(HALVES):
-                multiply(acc[:, h, :], w[h], v)
-            cols = slice(b * P, (b + 1) * P)
-            units.append((acc[:], bias_rows[:, cols].unsqueeze(1).to_broadcast([P, HALVES, P]), out_rows[:, :, cols]))
+                multiply(late[h][:, cols], w[h], v)
+        for h in range(HALVES):
+            units.append((late[h][:], bias_rows[:, 2 * P :], out_rows[:, h, 2 * P :]))
 
         for n, (acc, bias, dest) in enumerate(units):
             if n == 0:

from contextlib import ExitStack

import concourse.mybir as mybir
from concourse.masks import make_identity

F32 = mybir.dt.float32
BF16 = mybir.dt.bfloat16
U32 = mybir.dt.uint32
U16 = mybir.dt.uint16
U8 = mybir.dt.uint8
FP8X4 = mybir.dt.float8_e4m3fn_x4
SILU = mybir.ActivationFunctionType.Silu
ADD = mybir.AluOpType.add

P = 128
PACK = 4
SLOTS, TOKENS, QUERIES, FEATURES = 512, 2048, 256, 512
BLOCKS = FEATURES // P
HALVES = QUERIES // P
WINDOW_BYTES = TOKENS * 4
W_OFFSET = BLOCKS * WINDOW_BYTES

FLOPS = 2 * SLOTS * QUERIES * FEATURES


def tile_attend_wsum_silu_f_topk_kernel(tc, vT, wT, ob, offs, out):
    nc = tc.nc
    with ExitStack() as ctx:
        keep = ctx.enter_context(tc.tile_pool(name="keep", bufs=1))
        placed = ctx.enter_context(tc.tile_pool(name="placed", bufs=1))
        psum = ctx.enter_context(tc.psum_pool(name="psum", bufs=1))

        offsets = keep.tile([P, SLOTS // 16], U16, name="offsets")
        windows = [
            placed.tile([P, TOKENS], F32, name=f"window{b}", offset=b * WINDOW_BYTES, align_bytes=64)
            for b in range(BLOCKS)
        ]
        w_raw = placed.tile([P, PACK, QUERIES], F32, name="w_raw", offset=W_OFFSET, align_bytes=64)
        bias_col = keep.tile([P, PACK], F32, name="bias_col")

        nc.scalar.dma_start(bias_col[:], ob[0, 0].rearrange("(p c) -> p c", c=PACK))
        nc.sync.dma_start(windows[0][:], vT[0:P, :])
        nc.sync.dma_start(offsets[:], offs)
        for b in range(1, BLOCKS):
            nc.sync.dma_start(windows[b][:], vT[b * P : (b + 1) * P, :])
        nc.sync.dma_start(w_raw[:], wT[0].rearrange("(p j) q -> p j q", j=PACK))

        ident = keep.tile([P, P], F32, name="ident")
        make_identity(nc, ident[:])
        warm = keep.tile([P, 1], F32, name="warm")
        nc.scalar.activation(warm[:], ident[:, 0:1], SILU)

        bias_ps = psum.tile([P, PACK, P], F32, name="bias_ps")
        for c in range(PACK):
            nc.tensor.transpose(bias_ps[:, c, :], bias_col[:, c : c + 1].to_broadcast([P, P]), ident[:])
        bias_rows = keep.tile([P, FEATURES], F32, name="bias_rows")
        nc.scalar.copy(bias_rows[:].rearrange("q (n c) -> q n c", c=PACK), bias_ps[:].rearrange("q c n -> q n c"))

        def gather_and_turn(b, grouped):
            picked = keep.tile([P, 2, P, 2], BF16, name=f"picked{b}", align_bytes=64)
            nc.vector.tensor_copy(
                picked[:].rearrange("e u p v -> e p u v"), windows[b][:].indirect(offsets[:])
            )
            words = picked[:].rearrange("e u p v -> e (u p v)").bitcast(F32)
            turned = psum.tile([P, 2, P], F32, name=f"turned{b % 2}")
            for u in range(2):
                nc.tensor.transpose(turned[:, u, :], words[:, u * P : (u + 1) * P], ident[:])
            nc.scalar.copy(
                grouped.bitcast(F32).rearrange("p (e u) -> p e u", u=2),
                turned[:].rearrange("p u e -> p e u"),
            )

        def quantize(name, grouped, width, offset):
            if offset is None:
                codes = keep.tile([P, width], U32, name=f"{name}_codes", align_bytes=64)
            else:
                codes = placed.tile([P, width], U32, name=f"{name}_codes", offset=offset, align_bytes=64)
            scales = keep.tile([P, width], U8, name=f"{name}_scales", align_bytes=64)
            nc.vector.quantize_mx(out=codes[:].bitcast(FP8X4), scales=scales[:], in_=grouped)
            return codes, scales

        def multiply(acc, w, v):
            nc.tensor.matmul_mx(
                out=acc,
                lhsT=w[0][:].bitcast(FP8X4),
                lhsT_scale=w[1][:],
                rhs=v[0][:].bitcast(FP8X4),
                rhs_scale=v[1][:],
                start=True,
                stop=True,
            )

        grouped01 = keep.tile([P, 2 * P * PACK], BF16, name="grouped01", align_bytes=64)
        grouped2 = keep.tile([P, P * PACK], BF16, name="grouped2", align_bytes=64)
        gather_and_turn(0, grouped01[:, : P * PACK])
        gather_and_turn(1, grouped01[:, P * PACK :])
        gather_and_turn(2, grouped2[:])
        v01 = quantize("v01", grouped01[:], 2 * P, 2 * WINDOW_BYTES)

        w_grouped = [keep.tile([P, P, PACK], BF16, name=f"w_grouped{h}", align_bytes=64) for h in range(HALVES)]
        w_read = w_raw[:].rearrange("p j q -> p q j")
        for h, split in enumerate((80, 64)):
            nc.vector.tensor_copy(w_grouped[h][:, :split, :], w_read[:, h * P : h * P + split, :])
            nc.scalar.copy(w_grouped[h][:, split:, :], w_read[:, h * P + split : (h + 1) * P, :])

        grouped3 = placed.tile([P, P * PACK], BF16, name="grouped3", offset=W_OFFSET, align_bytes=64)
        gather_and_turn(3, grouped3[:])
        w = [quantize(f"w{h}", w_grouped[h][:].rearrange("p q j -> p (q j)"), P, None) for h in range(HALVES)]
        v2 = quantize("v2", grouped2[:], P, W_OFFSET + 2048)
        v3 = quantize("v3", grouped3[:], P, None)

        out_rows = out[0].rearrange("(h p) e -> p h e", p=P)
        units = []
        for h in range(HALVES):
            acc = psum.tile([P, 2 * P], F32, name=f"acc{h}")
            multiply(acc[:], w[h], v01)
            units.append((acc[:], bias_rows[:, : 2 * P], out_rows[:, h, : 2 * P]))
        late = [psum.tile([P, 2 * P], F32, name=f"late{h}") for h in range(HALVES)]
        for cols, v in ((slice(0, P), v2), (slice(P, 2 * P), v3)):
            for h in range(HALVES):
                multiply(late[h][:, cols], w[h], v)
        for h in range(HALVES):
            units.append((late[h][:], bias_rows[:, 2 * P :], out_rows[:, h, 2 * P :]))

        for n, (acc, bias, dest) in enumerate(units):
            if n == 0:
                summed = placed.tile(list(acc.shape), F32, name="summed0", offset=W_OFFSET, align_bytes=64)
            else:
                summed = keep.tile(list(acc.shape), F32, name=f"summed{n}")
            nc.vector.tensor_tensor(summed[:], acc, bias, ADD)
            result = keep.tile(list(acc.shape), F32, name=f"result{n}")
            nc.scalar.activation(result[:], summed[:], SILU)
            nc.sync.dma_start(dest, result[:])
